import numpy as np
import ml_dtypes


def mxq(x, axis, fmt="e4m3"):
    dtype, down = {"e4m3": (ml_dtypes.float8_e4m3fn, 7), "e5m2": (ml_dtypes.float8_e5m2, 14)}[fmt]
    v = np.moveaxis(np.asarray(x, np.float32).astype(ml_dtypes.bfloat16).astype(np.float64), axis, -1)
    blocks = v.reshape(v.shape[:-1] + (-1, 32))
    amax = np.abs(blocks).max(-1, keepdims=True)
    byte = np.maximum(np.where(amax > 0, np.frexp(amax)[1] - 1 + 127, 0) - down, 1)
    scale = np.exp2(byte - 127.0)
    codes = (blocks / scale).astype(np.float32).astype(dtype).astype(np.float64)
    return np.moveaxis((codes * scale).reshape(v.shape), -1, axis)


WIDE = False


def mx_kscale(k):
    if not WIDE:
        return np.ones(k)
    levels = np.array([10, -10, 5, -5, 0])
    if k % 512:
        return np.exp2(np.random.permutation(np.resize(levels, k // 32))).repeat(32)
    a = np.empty((k // 512, 16))
    for p in range(k // 512):
        a[p, :8] = np.random.permutation(np.resize(levels, 8))
        for g in range(8):
            far = levels[np.abs(levels - a[p, g]) >= 10]
            a[p, g + 8] = far[np.random.randint(len(far))]
    return np.exp2(a.ravel()).repeat(32)


BF16 = ml_dtypes.bfloat16


def bf(x):
    return np.asarray(x, np.float32).astype(BF16)


def f64(x):
    return np.asarray(x).astype(np.float64)


E2M1 = np.array([0.0, 0.5, 1.0, 1.5, 2.0, 3.0, 4.0, 6.0, -0.0, -0.5, -1.0, -1.5, -2.0, -3.0, -4.0, -6.0])


def pack_weight(w, fmt):
    k, n = w.shape
    w = f64(bf(w)).reshape(k // 32, 32, n)
    amax = np.abs(w).max(1)
    if fmt == "e4m3":
        byte = np.frexp(amax)[1] - 1 + 127 - 7
    else:
        mant, ex = np.frexp(amax / 6.0)
        byte = np.where(mant > 0.5, ex, ex - 1) + 127
    byte = np.clip(np.where(amax > 0, byte, 1), 1, 254)
    scaled = (w * np.exp2(127.0 - byte)[:, None, :]).reshape(k, n).astype(np.float32)
    by_word = np.ascontiguousarray(scaled.reshape(k // 512, 128, 4, n).transpose(0, 1, 3, 2))
    if fmt == "e4m3":
        words = by_word.astype(ml_dtypes.float8_e4m3fn).view(np.uint8)
    else:
        c = by_word.astype(ml_dtypes.float4_e2m1fn).view(np.uint8) & 0xF
        words = c[..., 0::2] | (c[..., 1::2] << 4)
    return np.ascontiguousarray(words), np.ascontiguousarray(byte.astype(np.uint8).reshape(k // 512, 16, n))


def unpack_weight(words, scales, fmt):
    g, p, n, _ = words.shape
    if fmt == "e4m3":
        vals = np.ascontiguousarray(words).view(ml_dtypes.float8_e4m3fn).astype(np.float64)
    else:
        nib = np.empty((g, p, n, 4), np.uint8)
        nib[..., 0::2] = words & 0xF
        nib[..., 1::2] = words >> 4
        vals = E2M1[nib]
    vals = vals * np.repeat(np.exp2(scales.astype(np.float64) - 127.0), 8, axis=1)[..., None]
    return vals.transpose(0, 1, 3, 2).reshape(g * 512, n)
def pack4(w):
    words, scales = pack_weight(w, "e2m1")
    return words.reshape(words.shape[0], 128, -1), scales


def unpack4(words, scales):
    return unpack_weight(words.reshape(words.shape[0], 128, -1, 2), scales, "e2m1")


def planes(Y):
    n, m = Y.shape
    b = f64(bf(Y)).reshape(n // 32, 32, m)
    amax = np.abs(b).max(1)
    byte = np.clip(np.where(amax > 0, np.frexp(amax)[1] - 1 + 127 - 7, 1), 1, 254)
    codes = (b * np.exp2(127.0 - byte)[:, None, :]).reshape(n, m).astype(np.float32).astype(ml_dtypes.float8_e4m3fn).view(np.uint8)
    words = codes.reshape(n // 512, 128, 4, m).transpose(0, 1, 3, 2)
    return np.ascontiguousarray(words), np.ascontiguousarray(byte.astype(np.uint8).reshape(n // 512, 16, m))


S, R, T, N = 896, 1024, 2048, 1536

def setup_inputs():
    s = mx_kscale(R)
    t = mx_kscale(T)
    shocks = np.random.randn(R, S) * s[:, None]
    sens = np.random.randn(R, T) / np.sqrt(R) / s[:, None] * t[None, :]
    x_words, x_scales = pack_weight(shocks, "e4m3")
    w_words, w_scales = pack4(sens)
    return {
        "x_words": x_words,
        "x_scales": x_scales,
        "w_words": w_words,
        "w_scales": w_scales,
        "base_value": bf(0.5 * np.random.randn(T) * t),
        "netting": bf(np.random.randn(T, N) / np.sqrt(T) / t[:, None]),
        "cash": bf(0.3 * np.random.randn(N)),
        "discount": bf(np.exp(-0.3 * np.abs(np.random.randn(S)))),
        "hedge_ratio": bf(np.exp(0.8 * np.random.randn(N))),
    }

def reference(x_words, x_scales, w_words, w_scales, base_value, netting, cash, discount, hedge_ratio):
    X = unpack_weight(x_words, x_scales, "e4m3")
    W = unpack4(w_words, w_scales)
    change = X.T @ W
    V = np.maximum(change + f64(base_value), 0.0)
    net = mxq(V, 1, "e4m3") @ mxq(f64(netting), 0, "e4m3")
    y = (net + f64(cash)) * f64(discount)[:, None] * f64(hedge_ratio)
    Y = y.T
    words, scales = planes(Y)
    return y, words, scales

@@ -1,0 +1,357 @@
+from contextlib import ExitStack
+
+import concourse.mybir as mybir
+from concourse.masks import make_identity
+
+S, R, T, N = 896, 1024, 2048, 1536
+FLOPS = 2 * S * R * T + 2 * S * T * N
+
+F32 = mybir.dt.float32
+BF16 = mybir.dt.bfloat16
+I32 = mybir.dt.int32
+U32 = mybir.dt.uint32
+U8 = mybir.dt.uint8
+FP8X4 = mybir.dt.float8_e4m3fn_x4
+FP4X4 = mybir.dt.float4_e2m1fn_x4
+ACT = mybir.ActivationFunctionType
+ALU = mybir.AluOpType
+
+P = 128
+KP = 512
+RG = R // KP
+TG = T // KP
+NG = N // KP
+CHUNKS = ((0, 512), (512, 384))
+STAGE1_WIDTHS = {512: (512,), 384: (128, 128, 128)}
+STAGE2_WIDTHS = {512: (512,), 384: (256, 128)}
+
+
+def windows(widths):
+    out = []
+    c = 0
+    for w in widths:
+        out.append((c, w))
+        c += w
+    return out
+
+
+def tile_shock_floor_netting_hedge_h2_kernel(
+    tc, x_words, x_scales, w_words, w_scales, base_value, netting, cash, discount, hedge_ratio, out_0, out_1, out_2
+):
+    nc = tc.nc
+    with ExitStack() as ctx:
+        keep = ctx.enter_context(tc.tile_pool(name="keep", bufs=1))
+        work = ctx.enter_context(tc.tile_pool(name="work", bufs=2))
+        psum = ctx.enter_context(tc.psum_pool(name="psum", bufs=4))
+        ctx.enter_context(tc.manual_schedule())
+
+        def kept(name, shape, dtype):
+            return keep.tile(shape, dtype, name=name, align_bytes=64)
+
+        def rotating(tag, bufs, shape, dtype):
+            return work.tile(shape, dtype, name=tag, tag=tag, bufs=bufs, align_bytes=64)
+
+        def bank(tag):
+            return psum.tile([P, 512], F32, name=tag, tag=tag)
+
+        x_codes = kept("x_codes", [P, RG, S], U32)
+        x_plane = kept("x_plane", [P, RG, S], U8)
+        w_raw = rotating("y", 2, [P, RG, T // 2], I32)
+        w_plane_raw = rotating("y_bf", 2, [P, RG, T], U8)
+        w_codes = kept("w_codes", [P, RG, 2 * T], U8)
+        w_plane = kept("w_plane", [P, RG, T], U8)
+        n_raw0 = kept("n_raw0", [P, TG, 4, KP], BF16)
+        n_raw12 = kept("n_raw12", [P, TG, 4, 2 * KP], BF16)
+        n_codes = kept("n_codes", [P, TG, N], U32)
+        n_plane = kept("n_plane", [P, TG, N], U8)
+        v_codes = kept("v_codes", [P, TG, S], U32)
+        v_plane = kept("v_plane", [P, TG, S], U8)
+        y_plane = kept("y_plane", [P, NG, S], U8)
+        rows = kept("rows", [P, KP], BF16)
+        rows_f32 = kept("rows_f32", [P, 4, P], F32)
+        cols = kept("cols", [P, 4, 16], F32)
+        ident = kept("ident", [P, P], F32)
+        hedge_bf = kept("hedge_bf", [P, NG, 4], BF16)
+        cash_bf = kept("cash_bf", [P, NG, 4], BF16)
+        hedge_col = kept("hedge_col", [P, NG, 4], F32)
+        cash_hedge = kept("cash_hedge", [P, NG, 4], F32)
+        disc_row = kept("disc_row", [P, S], BF16)
+        warm = kept("warm", [P, 2], F32)
+
+        nc.vector.memset(w_plane_raw[:].rearrange("p g c -> p (g c)").bitcast(I32), 0)
+        nc.vector.memset(x_plane[:].rearrange("p g c -> p (g c)").bitcast(I32), 0)
+        nc.vector.memset(warm[:, 0:1], 0.0)
+        nc.scalar.activation(out=warm[:, 1:2], in_=warm[:, 0:1], func=ACT.Relu)
+
+        nc.gpsimd.memset(rows[:], 0.0)
+        nc.gpsimd.dma_start(out=rows[0:TG, :], in_=base_value.rearrange("(k c) -> k c", k=TG))
+        nc.gpsimd.dma_start(
+            out=rows[TG : TG + S // P, :].rearrange("j (q t r) -> j q t r", t=4, r=8)[:, :, 0, :],
+            in_=discount.rearrange("(j q r) -> j q r", q=16, r=8),
+        )
+        make_identity(nc, ident[:])
+        nc.gpsimd.dma_start(out=hedge_bf[:], in_=hedge_ratio.rearrange("(g p t) -> p g t", p=P, t=4))
+        nc.gpsimd.dma_start(out=cash_bf[:], in_=cash.rearrange("(g p t) -> p g t", p=P, t=4))
+
+        w_src = w_words.rearrange("g p c -> p g c").bitcast(I32)
+        x_src = x_words.rearrange("g p n t -> p g (n t)").bitcast(I32)
+        nc.sync.dma_start(out=w_raw[:, :, 0:256], in_=w_src[:, :, 0:256])
+        nc.sync.dma_start(out=x_codes[:, :, 0:512].bitcast(I32), in_=x_src[:, :, 0:512])
+        for q in range(4):
+            nc.sync.dma_start(
+                out=w_plane_raw[32 * q : 32 * q + 4, :, :].bitcast(I32),
+                in_=w_scales[:, 4 * q : 4 * q + 4, :].rearrange("g r c -> r g c").bitcast(I32),
+            )
+        for q in range(4):
+            nc.sync.dma_start(
+                out=x_plane[32 * q : 32 * q + 4, :, :].bitcast(I32),
+                in_=x_scales[:, 4 * q : 4 * q + 4, :].rearrange("g r c -> r g c").bitcast(I32),
+            )
+        nc.sync.dma_start(out=w_raw[:, :, 256:1024], in_=w_src[:, :, 256:1024])
+        n_src = netting.rearrange("(k q t r) n -> k t q r n", q=16, t=4, r=8)
+        for k in range(TG):
+            for t in range(4):
+                nc.sync.dma_start(out=n_raw0[:, k, t, :], in_=n_src[k, t, :, :, 0:KP])
+        nc.sync.dma_start(out=x_codes[:, :, 512:S].bitcast(I32), in_=x_src[:, :, 512:S])
+        for k in range(TG):
+            for t in range(4):
+                nc.sync.dma_start(out=n_raw12[:, k, t, :], in_=n_src[k, t, :, :, KP:N])
+        nc.sync.dma_start(out=disc_row[:], in_=discount.partition_broadcast(P))
+
+        def permute_w(k):
+            nc.vector.tensor_copy(
+                out=w_codes[:].bitcast(I32)[:, :, 256 * k : 256 * (k + 1)].rearrange("p g (t q w) -> p g t q w", t=4, w=4),
+                in_=w_raw[:, :, 256 * k : 256 * (k + 1)].rearrange("p g (q t w) -> p g t q w", t=4, w=4),
+            )
+
+        permute_w(0)
+        nc.vector.tensor_copy(
+            out=w_plane[:].rearrange("p g c -> p (g c)").bitcast(I32).rearrange("p (k t q w) -> p k t q w", t=4, q=16, w=2),
+            in_=w_plane_raw[:].rearrange("p g c -> p (g c)").bitcast(I32).rearrange("p (k q t w) -> p k t q w", t=4, q=16, w=2),
+        )
+        nc.scalar.copy(
+            out=rows_f32[:].rearrange("p t (q r) -> p t q r", r=8),
+            in_=rows[:].rearrange("p (q t r) -> p t q r", t=4, r=8),
+        )
+        turned = bank("b")
+        for t in range(4):
+            nc.tensor.transpose(turned[:, P * t : P * (t + 1)], rows_f32[:, t, :], ident[:])
+        nc.scalar.copy(out=cols[:], in_=turned[:].rearrange("p (t c) -> p t c", t=4)[:, :, 0:16])
+        for k in range(1, TG):
+            permute_w(k)
+        nc.vector.tensor_copy(out=hedge_col[:], in_=hedge_bf[:])
+        nc.vector.tensor_tensor(out=cash_hedge[:], in0=cash_bf[:], in1=hedge_bf[:], op=ALU.mult)
+
+        v_rows = {}
+        staged = {}
+
+        def stage1(c, k):
+            s0, width = CHUNKS[c]
+            v_rows[c, k] = rotating("v_rows%d" % c, 3 + c, [P, 4, width], BF16)
+            for t in range(4):
+                acc = bank("ab"[t % 2])
+                col = 4 * k + t
+                for c0, w in windows(STAGE1_WIDTHS[width]):
+                    for g in range(RG):
+                        nc.tensor.matmul_mx(
+                            out=acc[:, c0 : c0 + w],
+                            lhsT=w_codes[:, g, 256 * col : 256 * (col + 1)].bitcast(FP4X4),
+                            lhsT_scale=w_plane[:, g, P * col : P * (col + 1)],
+                            rhs=x_codes[:, g, s0 + c0 : s0 + c0 + w].bitcast(FP8X4),
+                            rhs_scale=x_plane[:, g, s0 + c0 : s0 + c0 + w],
+                            start=(g == 0),
+                            stop=(g == RG - 1),
+                        )
+                nc.scalar.activation(
+                    out=v_rows[c, k][:, t, :], in_=acc[:, 0:width], func=ACT.Relu, bias=cols[:, t, k : k + 1]
+                )
+
+        def quantize(words, plane, grouped, width):
+            for c0, w in windows(STAGE2_WIDTHS[width]):
+                nc.vector.quantize_mx(
+                    out=words[:, c0 : c0 + w].bitcast(FP8X4),
+                    scales=plane[:, c0 : c0 + w],
+                    in_=grouped[:, c0 : c0 + w, :].rearrange("p s t -> p (s t)"),
+                )
+
+        def group_v(c, k):
+            width = CHUNKS[c][1]
+            staged["v", c, k] = rotating("v_grouped", 2, [P, width, 4], BF16)
+            nc.vector.tensor_copy(
+                out=staged["v", c, k][:].rearrange("p (a i) t -> p a t i", i=4),
+                in_=v_rows[c, k][:].rearrange("p t (a i) -> p a t i", i=4),
+            )
+
+        def quantize_v(c, k):
+            s0, width = CHUNKS[c]
+            quantize(v_codes[:, k, s0 : s0 + width], v_plane[:, k, s0 : s0 + width], staged["v", c, k], width)
+
+        def n_views(g, k, grouped, m0, m1):
+            raw = n_raw0[:, k, :, :] if g == 0 else n_raw12[:, k, :, KP * (g - 1) : KP * g]
+            dst = grouped[:].rearrange("p (u m) t -> p m u t", u=4)[:, m0:m1, :, :]
+            src = raw.rearrange("p t (m u) -> p m u t", u=4)[:, m0:m1, :, :]
+            return dst, src
+
+        def group_n(g, k):
+            staged["n", g, k] = rotating("n_grouped", 2, [P, KP, 4], BF16)
+            dst, src = n_views(g, k, staged["n", g, k], 0, P)
+            nc.vector.tensor_copy(out=dst, in_=src)
+
+        def group_n_quarter(g, k, quarter):
+            if quarter == 0:
+                staged["n", g, k] = rotating("n_grouped_scalar", 2, [P, KP, 4], BF16)
+            dst, src = n_views(g, k, staged["n", g, k], 32 * quarter, 32 * (quarter + 1))
+            nc.scalar.copy(out=dst, in_=src)
+
+        def quantize_n(g, k):
+            quantize(n_codes[:, k, KP * g : KP * (g + 1)], n_plane[:, k, KP * g : KP * (g + 1)], staged["n", g, k], KP)
+
+        units = [(g, c) for g in range(NG) for c in range(2)]
+        z = {}
+        y_words = {}
+
+        def stage2(u, t):
+            g, c = units[u]
+            s0, width = CHUNKS[c]
+            if t == 0:
+                z[u] = rotating("z%d" % c, 2, [P, 4, width], F32)
+            acc = bank("a")
+            col = KP * g + P * t
+            for c0, w in windows(STAGE2_WIDTHS[width]):
+                for k in range(TG):
+                    nc.tensor.matmul_mx(
+                        out=acc[:, c0 : c0 + w],
+                        lhsT=n_codes[:, k, col : col + P].bitcast(FP8X4),
+                        lhsT_scale=n_plane[:, k, col : col + P],
+                        rhs=v_codes[:, k, s0 + c0 : s0 + c0 + w].bitcast(FP8X4),
+                        rhs_scale=v_plane[:, k, s0 + c0 : s0 + c0 + w],
+                        start=(k == 0),
+                        stop=(k == TG - 1),
+                    )
+            nc.scalar.activation(
+                out=z[u][:, t, :],
+                in_=acc[:, 0:width],
+                func=ACT.Identity,
+                scale=hedge_col[:, g, t : t + 1],
+                bias=cash_hedge[:, g, t : t + 1],
+            )
+
+        def turn_and_store(u, queue):
+            g, c = units[u]
+            s0, width = CHUNKS[c]
+            tiles = width // P
+            y = rotating("y", 2, [P, tiles, KP], F32)
+            for j in range(tiles):
+                turned = bank("b")
+                for t in range(4):
+                    nc.tensor.transpose(turned[:, P * t : P * (t + 1)], z[u][:, t, P * j : P * (j + 1)], ident[:])
+                row = TG + s0 // P + j
+                nc.scalar.activation(
+                    out=y[:, j, :].rearrange("s (p t) -> s p t", t=4),
+                    in_=turned[:].rearrange("s (t p) -> s p t", t=4),
+                    func=ACT.Copy,
+                    scale=cols[:, 0, row : row + 1],
+                )
+            queue.dma_start(
+                out=out_0[s0 : s0 + width, KP * g : KP * (g + 1)].rearrange("(j s) n -> s j n", s=P), in_=y[:]
+            )
+
+        def group_y(u):
+            s0, width = CHUNKS[units[u][1]]
+            staged["y", u] = rotating("y_bf", 2, [P, width, 4], BF16)
+            nc.vector.tensor_tensor(
+                out=staged["y", u][:].rearrange("p (a i) t -> p a t i", i=4),
+                in0=z[u][:].rearrange("p t (a i) -> p a t i", i=4),
+                in1=disc_row[:, s0 : s0 + width].rearrange("p (a i) -> p a i", i=4).unsqueeze(2).to_broadcast([P, width // 4, 4, 4]),
+                op=ALU.mult,
+            )
+
+        def quantize_y(u):
+            g, c = units[u]
+            s0, width = CHUNKS[c]
+            y_words[u] = rotating("y_words", 3, [P, width], U32)
+            quantize(y_words[u][:], y_plane[:, g, s0 : s0 + width], staged["y", u], width)
+
+        def store_words(u):
+            g, c = units[u]
+            s0, width = CHUNKS[c]
+            nc.sync.dma_start(
+                out=out_1[g].rearrange("p s t -> p (s t)").bitcast(I32)[:, s0 : s0 + width], in_=y_words[u][:].bitcast(I32)
+            )
+
+        def store_scales(g0, g1, queues):
+            for q in range(4):
+                queues[q % len(queues)].dma_start(
+                    out=out_2[g0:g1, 4 * q : 4 * q + 4, :].rearrange("g r s -> r g s").bitcast(I32),
+                    in_=y_plane[32 * q : 32 * q + 4, g0:g1, :].bitcast(I32),
+                )
+
+        for k in range(TG):
+            stage1(0, k)
+            group_n(0, k)
+            group_v(0, k)
+            quantize_n(0, k)
+            quantize_v(0, k)
+        for k in range(TG):
+            stage1(1, k)
+        for k in range(TG):
+            group_v(1, k)
+            if k > 0:
+                quantize_v(1, k - 1)
+        group_n(1, 0)
+        quantize_v(1, TG - 1)
+
+        scalar_quarters = {
+            (0, 0): [(1, 3, 0)], (0, 1): [(1, 3, 1)], (0, 2): [(1, 3, 2)], (0, 3): [(1, 3, 3)],
+            (1, 1): [(2, 2, 0)], (1, 2): [(2, 2, 1)],
+            (2, 1): [(2, 2, 2)], (2, 2): [(2, 2, 3)], (2, 3): [(2, 3, 0), (2, 3, 1)],
+            (3, 1): [(2, 3, 2)], (3, 2): [(2, 3, 3)],
+        }
+
+        def unit(u):
+            for t in range(4):
+                stage2(u, t)
+                if t == 0 and u > 0:
+                    turn_and_store(u - 1, nc.sync)
+                for g, k, quarter in scalar_quarters.get((u, t), []):
+                    group_n_quarter(g, k, quarter)
+
+        unit(0)
+        group_n(1, 1)
+        quantize_n(1, 0)
+        group_n(1, 2)
+        quantize_n(1, 1)
+        quantize_n(1, 3)
+        quantize_n(1, 2)
+        group_y(0)
+        unit(1)
+        group_n(2, 0)
+        quantize_y(0)
+        group_n(2, 1)
+        quantize_n(2, 0)
+        quantize_n(2, 1)
+        unit(2)
+        store_words(0)
+        unit(3)
+        quantize_n(2, 2)
+        quantize_n(2, 3)
+        group_y(1)
+        group_y(2)
+        quantize_y(1)
+        group_y(3)
+        quantize_y(2)
+        store_words(1)
+        unit(4)
+        store_words(2)
+        group_y(4)
+        quantize_y(3)
+        quantize_y(4)
+        unit(5)
+        store_words(3)
+        store_scales(0, 2, [nc.sync])
+        store_words(4)
+        group_y(5)
+        quantize_y(5)
+        turn_and_store(5, nc.scalar)
+        store_words(5)
+        store_scales(2, 3, [nc.sync, nc.scalar])

@@ -23,7 +23,8 @@ TG = T // KP
 NG = N // KP
 CHUNKS = ((0, 512), (512, 384))
 STAGE1_WIDTHS = {512: (512,), 384: (128, 128, 128)}
-STAGE2_WIDTHS = {512: (512,), 384: (256, 128)}
+QUANTIZE_WORDS = {1024: (1024,), 768: (512, 256), 512: (512,), 384: (256, 128), 256: (256,), 128: (128,)}
+STAGE2_WIDTHS = {512: (512,), 384: (256, 128), 256: (256,), 128: (128,)}
 
 
 def windows(widths):
@@ -54,22 +55,25 @@ def tile_shock_floor_netting_hedge_h2_kernel(
         def bank(tag):
             return psum.tile([P, 512], F32, name=tag, tag=tag)
 
-        x_codes = kept("x_codes", [P, RG, S], U32)
+        x_codes = [kept("x_codes%d" % c, [P, RG, CHUNKS[c][1]], U32) for c in range(2)]
         x_plane = kept("x_plane", [P, RG, S], U8)
-        w_raw = rotating("y", 2, [P, RG, T // 2], I32)
+        w_raw = rotating("y", 2, [P, TG, RG, 256], I32)
         w_plane_raw = rotating("y_bf", 2, [P, RG, T], U8)
-        w_codes = kept("w_codes", [P, RG, 2 * T], U8)
+        w_codes = kept("w_codes", [P, TG, RG, 1024], U8)
         w_plane = kept("w_plane", [P, RG, T], U8)
-        n_raw0 = kept("n_raw0", [P, TG, 4, KP], BF16)
+        n_raw0 = [rotating("z_wide", 2, [P, 2, 4, KP], BF16) for half in range(2)]
         n_raw12 = kept("n_raw12", [P, TG, 4, 2 * KP], BF16)
-        n_codes = kept("n_codes", [P, TG, N], U32)
-        n_plane = kept("n_plane", [P, TG, N], U8)
-        v_codes = kept("v_codes", [P, TG, S], U32)
-        v_plane = kept("v_plane", [P, TG, S], U8)
+        n_codes = kept("n_codes", [P, NG, TG, KP], U32)
+        n_plane = kept("n_plane", [P, NG, TG, KP], U8)
+        v_codes = [kept("v_codes%d" % c, [P, TG, CHUNKS[c][1]], U32) for c in range(2)]
+        v_plane = [kept("v_plane%d" % c, [P, TG, CHUNKS[c][1]], U8) for c in range(2)]
         y_plane = kept("y_plane", [P, NG, S], U8)
         rows = kept("rows", [P, KP], BF16)
-        rows_f32 = kept("rows_f32", [P, 4, P], F32)
-        cols = kept("cols", [P, 4, 16], F32)
+        rows_f32 = rotating("y_last", 1, [P, 4, P], F32)
+        cols = kept("cols", [P, 4, TG], F32)
+        disc_rows = kept("disc_rows", [P, P], BF16)
+        disc_rows_f32 = kept("disc_rows_f32", [P, P], F32)
+        disc_col = kept("disc_col", [P, 8], F32)
         ident = kept("ident", [P, P], F32)
         hedge_bf = kept("hedge_bf", [P, NG, 4], BF16)
         cash_bf = kept("cash_bf", [P, NG, 4], BF16)
@@ -80,74 +84,94 @@ def tile_shock_floor_netting_hedge_h2_kernel(
 
         nc.vector.memset(w_plane_raw[:].rearrange("p g c -> p (g c)").bitcast(I32), 0)
         nc.vector.memset(x_plane[:].rearrange("p g c -> p (g c)").bitcast(I32), 0)
-        nc.vector.memset(warm[:, 0:1], 0.0)
+        nc.gpsimd.memset(warm[:, 0:1], 0.0)
         nc.scalar.activation(out=warm[:, 1:2], in_=warm[:, 0:1], func=ACT.Relu)
 
         nc.gpsimd.memset(rows[:], 0.0)
         nc.gpsimd.dma_start(out=rows[0:TG, :], in_=base_value.rearrange("(k c) -> k c", k=TG))
-        nc.gpsimd.dma_start(
-            out=rows[TG : TG + S // P, :].rearrange("j (q t r) -> j q t r", t=4, r=8)[:, :, 0, :],
-            in_=discount.rearrange("(j q r) -> j q r", q=16, r=8),
-        )
         make_identity(nc, ident[:])
-        nc.gpsimd.dma_start(out=hedge_bf[:], in_=hedge_ratio.rearrange("(g p t) -> p g t", p=P, t=4))
-        nc.gpsimd.dma_start(out=cash_bf[:], in_=cash.rearrange("(g p t) -> p g t", p=P, t=4))
+        nc.gpsimd.memset(disc_rows[:], 0.0)
 
         w_src = w_words.rearrange("g p c -> p g c").bitcast(I32)
         x_src = x_words.rearrange("g p n t -> p g (n t)").bitcast(I32)
-        nc.sync.dma_start(out=w_raw[:, :, 0:256], in_=w_src[:, :, 0:256])
-        nc.sync.dma_start(out=x_codes[:, :, 0:512].bitcast(I32), in_=x_src[:, :, 0:512])
-        for q in range(4):
-            nc.sync.dma_start(
-                out=w_plane_raw[32 * q : 32 * q + 4, :, :].bitcast(I32),
-                in_=w_scales[:, 4 * q : 4 * q + 4, :].rearrange("g r c -> r g c").bitcast(I32),
-            )
-        for q in range(4):
-            nc.sync.dma_start(
-                out=x_plane[32 * q : 32 * q + 4, :, :].bitcast(I32),
-                in_=x_scales[:, 4 * q : 4 * q + 4, :].rearrange("g r c -> r g c").bitcast(I32),
-            )
-        nc.sync.dma_start(out=w_raw[:, :, 256:1024], in_=w_src[:, :, 256:1024])
         n_src = netting.rearrange("(k q t r) n -> k t q r n", q=16, t=4, r=8)
-        for k in range(TG):
+
+        def load_w(k):
+            nc.sync.dma_start(out=w_raw[:, k, :, :], in_=w_src[:, :, 256 * k : 256 * (k + 1)])
+
+        def load_x(c):
+            s0, width = CHUNKS[c]
+            nc.sync.dma_start(out=x_codes[c][:].bitcast(I32), in_=x_src[:, :, s0 : s0 + width])
+
+        def load_plane(plane, scales):
+            for r in range(4):
+                nc.sync.dma_start(
+                    out=plane[r:P:32, :, :].bitcast(I32),
+                    in_=scales[:, r:16:4, :].rearrange("g q c -> q g c").bitcast(I32),
+                )
+
+        def load_n(raw, k, n0, n1):
             for t in range(4):
-                nc.sync.dma_start(out=n_raw0[:, k, t, :], in_=n_src[k, t, :, :, 0:KP])
-        nc.sync.dma_start(out=x_codes[:, :, 512:S].bitcast(I32), in_=x_src[:, :, 512:S])
+                nc.sync.dma_start(out=raw[:, t, :], in_=n_src[k, t, :, :, n0:n1])
+
+        load_n(n_raw0[0][:, 0, :, :], 0, 0, KP)
+        load_x(0)
+        load_w(0)
+        load_plane(w_plane_raw, w_scales)
+        load_plane(x_plane, x_scales)
+        load_w(1)
+        load_n(n_raw0[0][:, 1, :, :], 1, 0, KP)
+        load_w(2)
+        load_w(3)
+        load_n(n_raw0[1][:, 0, :, :], 2, 0, KP)
+        load_n(n_raw0[1][:, 1, :, :], 3, 0, KP)
+        load_x(1)
+        nc.sync.dma_start(out=hedge_bf[:], in_=hedge_ratio.rearrange("(g p t) -> p g t", p=P, t=4))
+        nc.sync.dma_start(out=cash_bf[:], in_=cash.rearrange("(g p t) -> p g t", p=P, t=4))
+        nc.sync.dma_start(out=disc_rows[0 : S // P, :], in_=discount.rearrange("(j c) -> j c", c=P))
         for k in range(TG):
-            for t in range(4):
-                nc.sync.dma_start(out=n_raw12[:, k, t, :], in_=n_src[k, t, :, :, KP:N])
+            load_n(n_raw12[:, k, :, :], k, KP, N)
         nc.sync.dma_start(out=disc_row[:], in_=discount.partition_broadcast(P))
 
-        def permute_w(k):
+        def permute_w(k0, k1):
             nc.vector.tensor_copy(
-                out=w_codes[:].bitcast(I32)[:, :, 256 * k : 256 * (k + 1)].rearrange("p g (t q w) -> p g t q w", t=4, w=4),
-                in_=w_raw[:, :, 256 * k : 256 * (k + 1)].rearrange("p g (q t w) -> p g t q w", t=4, w=4),
+                out=w_codes[:, k0:k1, :, :].bitcast(I32).rearrange("p k g (t q w) -> p (k g) t q w", t=4, w=4),
+                in_=w_raw[:, k0:k1, :, :].rearrange("p k g (q t w) -> p (k g) t q w", t=4, w=4),
             )
 
-        permute_w(0)
-        nc.vector.tensor_copy(
-            out=w_plane[:].rearrange("p g c -> p (g c)").bitcast(I32).rearrange("p (k t q w) -> p k t q w", t=4, q=16, w=2),
-            in_=w_plane_raw[:].rearrange("p g c -> p (g c)").bitcast(I32).rearrange("p (k q t w) -> p k t q w", t=4, q=16, w=2),
-        )
-        nc.scalar.copy(
-            out=rows_f32[:].rearrange("p t (q r) -> p t q r", r=8),
-            in_=rows[:].rearrange("p (q t r) -> p t q r", t=4, r=8),
-        )
-        turned = bank("b")
-        for t in range(4):
-            nc.tensor.transpose(turned[:, P * t : P * (t + 1)], rows_f32[:, t, :], ident[:])
-        nc.scalar.copy(out=cols[:], in_=turned[:].rearrange("p (t c) -> p t c", t=4)[:, :, 0:16])
-        for k in range(1, TG):
-            permute_w(k)
-        nc.vector.tensor_copy(out=hedge_col[:], in_=hedge_bf[:])
-        nc.vector.tensor_tensor(out=cash_hedge[:], in0=cash_bf[:], in1=hedge_bf[:], op=ALU.mult)
+        def permute_w_plane():
+            nc.vector.tensor_copy(
+                out=w_plane[:].rearrange("p g c -> p (g c)").bitcast(I32).rearrange("p (k t q w) -> p k t q w", t=4, q=16, w=2),
+                in_=w_plane_raw[:].rearrange("p g c -> p (g c)").bitcast(I32).rearrange("p (k q t w) -> p k t q w", t=4, q=16, w=2),
+            )
+
+        def turn_vectors():
+            nc.vector.tensor_copy(
+                out=rows_f32[:].rearrange("p t (q r) -> p t q r", r=8),
+                in_=rows[:].rearrange("p (q t r) -> p t q r", t=4, r=8),
+            )
+            turned = bank("b")
+            for t in range(4):
+                nc.tensor.transpose(turned[:, P * t : P * (t + 1)], rows_f32[:, t, :], ident[:])
+            nc.scalar.copy(out=cols[:], in_=turned[:].rearrange("p (t c) -> p t c", t=4)[:, :, 0:TG])
+
+        def turn_discount():
+            turned = bank("a")
+            nc.tensor.transpose(turned[:, 0:P], disc_rows_f32[:], ident[:])
+            nc.scalar.copy(out=disc_col[:], in_=turned[:, 0:8])
+
+        def hedge_columns():
+            nc.vector.tensor_copy(out=disc_rows_f32[:], in_=disc_rows[:])
+            nc.vector.tensor_copy(out=hedge_col[:], in_=hedge_bf[:])
+            nc.vector.tensor_tensor(out=cash_hedge[:], in0=cash_bf[:], in1=hedge_bf[:], op=ALU.mult)
 
         v_rows = {}
         staged = {}
 
         def stage1(c, k):
             s0, width = CHUNKS[c]
-            v_rows[c, k] = rotating("v_rows%d" % c, 3 + c, [P, 4, width], BF16)
+            if k % 2 == 0:
+                v_rows[c, k // 2] = rotating("v_rows%d" % c, 2, [P, 2, 4, width], BF16)
             for t in range(4):
                 acc = bank("ab"[t % 2])
                 col = 4 * k + t
@@ -155,76 +179,87 @@ def tile_shock_floor_netting_hedge_h2_kernel(
                     for g in range(RG):
                         nc.tensor.matmul_mx(
                             out=acc[:, c0 : c0 + w],
-                            lhsT=w_codes[:, g, 256 * col : 256 * (col + 1)].bitcast(FP4X4),
+                            lhsT=w_codes[:, k, g, 256 * t : 256 * (t + 1)].bitcast(FP4X4),
                             lhsT_scale=w_plane[:, g, P * col : P * (col + 1)],
-                            rhs=x_codes[:, g, s0 + c0 : s0 + c0 + w].bitcast(FP8X4),
+                            rhs=x_codes[c][:, g, c0 : c0 + w].bitcast(FP8X4),
                             rhs_scale=x_plane[:, g, s0 + c0 : s0 + c0 + w],
                             start=(g == 0),
                             stop=(g == RG - 1),
                         )
                 nc.scalar.activation(
-                    out=v_rows[c, k][:, t, :], in_=acc[:, 0:width], func=ACT.Relu, bias=cols[:, t, k : k + 1]
+                    out=v_rows[c, k // 2][:, k % 2, t, :], in_=acc[:, 0:width], func=ACT.Relu, bias=cols[:, t, k : k + 1]
                 )
 
-        def quantize(words, plane, grouped, width):
-            for c0, w in windows(STAGE2_WIDTHS[width]):
+        def quantize(words, plane, grouped):
+            for c0, w in windows(QUANTIZE_WORDS[words.shape[1]]):
                 nc.vector.quantize_mx(
                     out=words[:, c0 : c0 + w].bitcast(FP8X4),
                     scales=plane[:, c0 : c0 + w],
-                    in_=grouped[:, c0 : c0 + w, :].rearrange("p s t -> p (s t)"),
+                    in_=grouped[:, 4 * c0 : 4 * (c0 + w)],
                 )
 
-        def group_v(c, k):
+        def group_v(c, h):
             width = CHUNKS[c][1]
-            staged["v", c, k] = rotating("v_grouped", 2, [P, width, 4], BF16)
+            staged["v", c, h] = rotating("grouped", 4, [P, 2, width, 4], BF16)
             nc.vector.tensor_copy(
-                out=staged["v", c, k][:].rearrange("p (a i) t -> p a t i", i=4),
-                in_=v_rows[c, k][:].rearrange("p t (a i) -> p a t i", i=4),
+                out=staged["v", c, h][:].rearrange("p k (a i) t -> p k a t i", i=4),
+                in_=v_rows[c, h][:].rearrange("p k t (a i) -> p k a t i", i=4),
             )
 
-        def quantize_v(c, k):
-            s0, width = CHUNKS[c]
-            quantize(v_codes[:, k, s0 : s0 + width], v_plane[:, k, s0 : s0 + width], staged["v", c, k], width)
+        def quantize_v(c, h):
+            quantize(
+                v_codes[c][:, 2 * h : 2 * h + 2, :].rearrange("p k s -> p (k s)"),
+                v_plane[c][:, 2 * h : 2 * h + 2, :].rearrange("p k s -> p (k s)"),
+                staged["v", c, h][:].rearrange("p k s t -> p (k s t)"),
+            )
 
-        def n_views(g, k, grouped, m0, m1):
-            raw = n_raw0[:, k, :, :] if g == 0 else n_raw12[:, k, :, KP * (g - 1) : KP * g]
-            dst = grouped[:].rearrange("p (u m) t -> p m u t", u=4)[:, m0:m1, :, :]
-            src = raw.rearrange("p t (m u) -> p m u t", u=4)[:, m0:m1, :, :]
+        def n_views(g, h):
+            if ("n", g, h) not in staged:
+                staged["n", g, h] = rotating("grouped", 4, [P, 2, KP, 4], BF16)
+            raw = n_raw0[h][:] if g == 0 else n_raw12[:, 2 * h : 2 * h + 2, :, KP * (g - 1) : KP * g]
+            dst = staged["n", g, h][:].rearrange("p k (u m) t -> p k m u t", u=4)
+            src = raw.rearrange("p k t (m u) -> p k m u t", u=4)
             return dst, src
 
-        def group_n(g, k):
-            staged["n", g, k] = rotating("n_grouped", 2, [P, KP, 4], BF16)
-            dst, src = n_views(g, k, staged["n", g, k], 0, P)
+        def group_n_pair(g, h):
+            dst, src = n_views(g, h)
             nc.vector.tensor_copy(out=dst, in_=src)
 
+        def group_n(g, k):
+            dst, src = n_views(g, k // 2)
+            nc.vector.tensor_copy(out=dst[:, k % 2, :, :, :], in_=src[:, k % 2, :, :, :])
+
         def group_n_quarter(g, k, quarter):
-            if quarter == 0:
-                staged["n", g, k] = rotating("n_grouped_scalar", 2, [P, KP, 4], BF16)
-            dst, src = n_views(g, k, staged["n", g, k], 32 * quarter, 32 * (quarter + 1))
-            nc.scalar.copy(out=dst, in_=src)
+            dst, src = n_views(g, k // 2)
+            m = slice(32 * quarter, 32 * (quarter + 1))
+            nc.scalar.copy(out=dst[:, k % 2, m, :, :], in_=src[:, k % 2, m, :, :])
 
-        def quantize_n(g, k):
-            quantize(n_codes[:, k, KP * g : KP * (g + 1)], n_plane[:, k, KP * g : KP * (g + 1)], staged["n", g, k], KP)
+        def quantize_n(g, h):
+            quantize(
+                n_codes[:, g, 2 * h : 2 * h + 2, :].rearrange("p k n -> p (k n)"),
+                n_plane[:, g, 2 * h : 2 * h + 2, :].rearrange("p k n -> p (k n)"),
+                staged["n", g, h][:].rearrange("p k n t -> p (k n t)"),
+            )
 
-        units = [(g, c) for g in range(NG) for c in range(2)]
+        units = [(0, 0, 512), (0, 512, 384), (1, 0, 512), (1, 512, 384), (2, 0, 512), (2, 512, 256), (2, 768, 128)]
         z = {}
         y_words = {}
 
         def stage2(u, t):
-            g, c = units[u]
-            s0, width = CHUNKS[c]
+            g, s0, width = units[u]
             if t == 0:
-                z[u] = rotating("z%d" % c, 2, [P, 4, width], F32)
+                z[u] = rotating({512: "z_wide", 128: "z_last"}.get(width, "z_narrow"), 1 if width == P else 2, [P, 4, width], F32)
             acc = bank("a")
-            col = KP * g + P * t
+            c = s0 // KP
+            c1 = s0 - CHUNKS[c][0]
             for c0, w in windows(STAGE2_WIDTHS[width]):
                 for k in range(TG):
                     nc.tensor.matmul_mx(
                         out=acc[:, c0 : c0 + w],
-                        lhsT=n_codes[:, k, col : col + P].bitcast(FP8X4),
-                        lhsT_scale=n_plane[:, k, col : col + P],
-                        rhs=v_codes[:, k, s0 + c0 : s0 + c0 + w].bitcast(FP8X4),
-                        rhs_scale=v_plane[:, k, s0 + c0 : s0 + c0 + w],
+                        lhsT=n_codes[:, g, k, P * t : P * (t + 1)].bitcast(FP8X4),
+                        lhsT_scale=n_plane[:, g, k, P * t : P * (t + 1)],
+                        rhs=v_codes[c][:, k, c1 + c0 : c1 + c0 + w].bitcast(FP8X4),
+                        rhs_scale=v_plane[c][:, k, c1 + c0 : c1 + c0 + w],
                         start=(k == 0),
                         stop=(k == TG - 1),
                     )
@@ -236,28 +271,47 @@ def tile_shock_floor_netting_hedge_h2_kernel(
                 bias=cash_hedge[:, g, t : t + 1],
             )
 
-        def turn_and_store(u, queue):
-            g, c = units[u]
-            s0, width = CHUNKS[c]
-            tiles = width // P
-            y = rotating("y", 2, [P, tiles, KP], F32)
-            for j in range(tiles):
-                turned = bank("b")
+        turned_z = {}
+        y_rows = {}
+
+        def turn(u):
+            width = units[u][2]
+            for j in range(width // P):
+                turned_z[u, j] = bank("b")
                 for t in range(4):
-                    nc.tensor.transpose(turned[:, P * t : P * (t + 1)], z[u][:, t, P * j : P * (j + 1)], ident[:])
-                row = TG + s0 // P + j
-                nc.scalar.activation(
-                    out=y[:, j, :].rearrange("s (p t) -> s p t", t=4),
-                    in_=turned[:].rearrange("s (t p) -> s p t", t=4),
-                    func=ACT.Copy,
-                    scale=cols[:, 0, row : row + 1],
+                    nc.tensor.transpose(turned_z[u, j][:, P * t : P * (t + 1)], z[u][:, t, P * j : P * (j + 1)], ident[:])
+
+        def discount_tile(u, j, on_vector=False):
+            g, s0, width = units[u]
+            if j == 0:
+                y_rows[u] = rotating("y" if width > P else "y_last", 2 if width > P else 1, [P, width // P, KP], F32)
+            natural = y_rows[u][:, j, :].rearrange("s (p t) -> s p t", t=4)
+            by_slot = turned_z[u, j][:].rearrange("s (t p) -> s p t", t=4)
+            row = s0 // P + j
+            if on_vector:
+                nc.vector.tensor_scalar(
+                    out=natural, in0=by_slot, scalar1=disc_col[:, row : row + 1], scalar2=None, op0=ALU.mult
                 )
+            else:
+                nc.scalar.activation(out=natural, in_=by_slot, func=ACT.Copy, scale=disc_col[:, row : row + 1])
+
+        def store_rows(u, j0, j1, queue):
+            g, s0, width = units[u]
             queue.dma_start(
-                out=out_0[s0 : s0 + width, KP * g : KP * (g + 1)].rearrange("(j s) n -> s j n", s=P), in_=y[:]
+                out=out_0[s0 + P * j0 : s0 + P * j1, KP * g : KP * (g + 1)].rearrange("(j s) n -> s j n", s=P),
+                in_=y_rows[u][:, j0:j1, :],
             )
 
+        def turn_and_store(u):
+            tiles = units[u][2] // P
+            turn(u)
+            for j in range(tiles):
+                discount_tile(u, j)
+                if j % 2 == 1 or j == tiles - 1:
+                    store_rows(u, j - j % 2, j + 1, nc.sync)
+
         def group_y(u):
-            s0, width = CHUNKS[units[u][1]]
+            g, s0, width = units[u]
             staged["y", u] = rotating("y_bf", 2, [P, width, 4], BF16)
             nc.vector.tensor_tensor(
                 out=staged["y", u][:].rearrange("p (a i) t -> p a t i", i=4),
@@ -267,14 +321,12 @@ def tile_shock_floor_netting_hedge_h2_kernel(
             )
 
         def quantize_y(u):
-            g, c = units[u]
-            s0, width = CHUNKS[c]
-            y_words[u] = rotating("y_words", 3, [P, width], U32)
-            quantize(y_words[u][:], y_plane[:, g, s0 : s0 + width], staged["y", u], width)
+            g, s0, width = units[u]
+            y_words[u] = rotating("y_words", 4, [P, width], U32)
+            quantize(y_words[u][:], y_plane[:, g, s0 : s0 + width], staged["y", u][:].rearrange("p s t -> p (s t)"))
 
         def store_words(u):
-            g, c = units[u]
-            s0, width = CHUNKS[c]
+            g, s0, width = units[u]
             nc.sync.dma_start(
                 out=out_1[g].rearrange("p s t -> p (s t)").bitcast(I32)[:, s0 : s0 + width], in_=y_words[u][:].bitcast(I32)
             )
@@ -286,72 +338,105 @@ def tile_shock_floor_netting_hedge_h2_kernel(
                     in_=y_plane[32 * q : 32 * q + 4, g0:g1, :].bitcast(I32),
                 )
 
-        for k in range(TG):
-            stage1(0, k)
-            group_n(0, k)
-            group_v(0, k)
-            quantize_n(0, k)
-            quantize_v(0, k)
+        for quarter in range(4):
+            group_n_quarter(0, 0, quarter)
+        turn_vectors()
+        permute_w(0, 1)
+        permute_w_plane()
+        stage1(0, 0)
+        permute_w(1, 2)
+        stage1(0, 1)
+        group_n(0, 1)
+        permute_w(2, 4)
+        quantize_n(0, 0)
+        group_n(0, 2)
+        stage1(0, 2)
+        group_v(0, 0)
+        group_n(0, 3)
+        quantize_v(0, 0)
+        stage1(0, 3)
+        group_v(0, 1)
+        quantize_n(0, 1)
+        hedge_columns()
+        quantize_v(0, 1)
         for k in range(TG):
             stage1(1, k)
-        for k in range(TG):
-            group_v(1, k)
-            if k > 0:
-                quantize_v(1, k - 1)
-        group_n(1, 0)
-        quantize_v(1, TG - 1)
+        group_v(1, 0)
+        group_v(1, 1)
+        quantize_v(1, 0)
+        quantize_v(1, 1)
 
         scalar_quarters = {
-            (0, 0): [(1, 3, 0)], (0, 1): [(1, 3, 1)], (0, 2): [(1, 3, 2)], (0, 3): [(1, 3, 3)],
-            (1, 1): [(2, 2, 0)], (1, 2): [(2, 2, 1)],
-            (2, 1): [(2, 2, 2)], (2, 2): [(2, 2, 3)], (2, 3): [(2, 3, 0), (2, 3, 1)],
-            (3, 1): [(2, 3, 2)], (3, 2): [(2, 3, 3)],
+            (0, 0): [(1, 0, 0)], (0, 1): [(1, 0, 1)], (0, 2): [(1, 0, 2)], (0, 3): [(1, 0, 3)],
+            (1, 1): [(2, 0, 0)], (1, 2): [(2, 0, 1)], (1, 3): [(2, 0, 2), (2, 0, 3)],
         }
 
         def unit(u):
             for t in range(4):
                 stage2(u, t)
-                if t == 0 and u > 0:
-                    turn_and_store(u - 1, nc.sync)
+                if (u, t) == (1, 0):
+                    turn_discount()
+                if t == 0 and 0 < u < 5:
+                    turn_and_store(u - 1)
                 for g, k, quarter in scalar_quarters.get((u, t), []):
                     group_n_quarter(g, k, quarter)
 
         unit(0)
+        group_n_pair(1, 1)
         group_n(1, 1)
-        quantize_n(1, 0)
-        group_n(1, 2)
         quantize_n(1, 1)
-        quantize_n(1, 3)
-        quantize_n(1, 2)
-        group_y(0)
+        quantize_n(1, 0)
         unit(1)
-        group_n(2, 0)
-        quantize_y(0)
+        group_n_pair(2, 1)
+        group_y(0)
         group_n(2, 1)
-        quantize_n(2, 0)
         quantize_n(2, 1)
+        quantize_n(2, 0)
+        quantize_y(0)
         unit(2)
         store_words(0)
-        unit(3)
-        quantize_n(2, 2)
-        quantize_n(2, 3)
         group_y(1)
         group_y(2)
         quantize_y(1)
+        unit(3)
         group_y(3)
         quantize_y(2)
         store_words(1)
         unit(4)
         store_words(2)
-        group_y(4)
         quantize_y(3)
+        group_y(4)
         quantize_y(4)
-        unit(5)
         store_words(3)
         store_scales(0, 2, [nc.sync])
+        stage2(5, 0)
+        turn(4)
+        discount_tile(4, 0)
+        discount_tile(4, 1)
+        store_rows(4, 0, 2, nc.sync)
+        discount_tile(4, 2)
+        stage2(5, 1)
+        discount_tile(4, 3)
+        store_rows(4, 2, 4, nc.sync)
+        stage2(5, 2)
+        stage2(5, 3)
         store_words(4)
         group_y(5)
+        stage2(6, 0)
+        stage2(6, 1)
+        stage2(6, 2)
+        stage2(6, 3)
+        turn(5)
+        turn(6)
+        group_y(6)
         quantize_y(5)
-        turn_and_store(5, nc.scalar)
+        quantize_y(6)
+        discount_tile(5, 0)
+        store_rows(5, 0, 1, nc.sync)
+        discount_tile(5, 1)
+        discount_tile(6, 0)
         store_words(5)
+        store_rows(5, 1, 2, nc.sync)
+        store_rows(6, 0, 1, nc.scalar)
+        store_words(6)
         store_scales(2, 3, [nc.sync, nc.scalar])

@@ -62,7 +62,7 @@ def tile_shock_floor_netting_hedge_h2_kernel(
         w_codes = kept("w_codes", [P, TG, RG, 1024], U8)
         w_plane = kept("w_plane", [P, RG, T], U8)
         n_raw0 = [rotating("z_wide", 2, [P, 2, 4, KP], BF16) for half in range(2)]
-        n_raw12 = kept("n_raw12", [P, TG, 4, 2 * KP], BF16)
+        n_raw12 = kept("n_raw12", [P, NG - 1, TG, 4, KP], BF16)
         n_codes = kept("n_codes", [P, NG, TG, KP], U32)
         n_plane = kept("n_plane", [P, NG, TG, KP], U8)
         v_codes = [kept("v_codes%d" % c, [P, TG, CHUNKS[c][1]], U32) for c in range(2)]
@@ -82,26 +82,24 @@ def tile_shock_floor_netting_hedge_h2_kernel(
         disc_row = kept("disc_row", [P, S], BF16)
         warm = kept("warm", [P, 2], F32)
 
+        nc.vector.memset(rows[:], 0.0)
+        nc.vector.memset(warm[:, 0:1], 0.0)
+        nc.scalar.dma_start(out=rows[0:TG, :], in_=base_value.rearrange("(k c) -> k c", k=TG))
+        nc.scalar.activation(out=warm[:, 1:2], in_=warm[:, 0:1], func=ACT.Relu)
         nc.vector.memset(w_plane_raw[:].rearrange("p g c -> p (g c)").bitcast(I32), 0)
         nc.vector.memset(x_plane[:].rearrange("p g c -> p (g c)").bitcast(I32), 0)
-        nc.gpsimd.memset(warm[:, 0:1], 0.0)
-        nc.scalar.activation(out=warm[:, 1:2], in_=warm[:, 0:1], func=ACT.Relu)
 
-        nc.gpsimd.memset(rows[:], 0.0)
-        nc.gpsimd.dma_start(out=rows[0:TG, :], in_=base_value.rearrange("(k c) -> k c", k=TG))
-        make_identity(nc, ident[:])
-        nc.gpsimd.memset(disc_rows[:], 0.0)
 
         w_src = w_words.rearrange("g p c -> p g c").bitcast(I32)
         x_src = x_words.rearrange("g p n t -> p g (n t)").bitcast(I32)
         n_src = netting.rearrange("(k q t r) n -> k t q r n", q=16, t=4, r=8)
 
-        def load_w(k):
-            nc.sync.dma_start(out=w_raw[:, k, :, :], in_=w_src[:, :, 256 * k : 256 * (k + 1)])
+        def load_w(k, queue):
+            queue.dma_start(out=w_raw[:, k, :, :], in_=w_src[:, :, 256 * k : 256 * (k + 1)])
 
-        def load_x(c):
+        def load_x(c, queue):
             s0, width = CHUNKS[c]
-            nc.sync.dma_start(out=x_codes[c][:].bitcast(I32), in_=x_src[:, :, s0 : s0 + width])
+            queue.dma_start(out=x_codes[c][:].bitcast(I32), in_=x_src[:, :, s0 : s0 + width])
 
         def load_plane(plane, scales):
             for r in range(4):
@@ -115,23 +113,27 @@ def tile_shock_floor_netting_hedge_h2_kernel(
                 nc.sync.dma_start(out=raw[:, t, :], in_=n_src[k, t, :, :, n0:n1])
 
         load_n(n_raw0[0][:, 0, :, :], 0, 0, KP)
-        load_x(0)
-        load_w(0)
+        load_x(0, nc.gpsimd)
+        load_w(0, nc.gpsimd)
+        make_identity(nc, ident[:])
+        nc.gpsimd.memset(disc_rows[:], 0.0)
         load_plane(w_plane_raw, w_scales)
         load_plane(x_plane, x_scales)
-        load_w(1)
         load_n(n_raw0[0][:, 1, :, :], 1, 0, KP)
-        load_w(2)
-        load_w(3)
+        load_w(1, nc.sync)
+        load_w(2, nc.sync)
         load_n(n_raw0[1][:, 0, :, :], 2, 0, KP)
+        load_w(3, nc.sync)
         load_n(n_raw0[1][:, 1, :, :], 3, 0, KP)
-        load_x(1)
+        load_x(1, nc.sync)
         nc.sync.dma_start(out=hedge_bf[:], in_=hedge_ratio.rearrange("(g p t) -> p g t", p=P, t=4))
         nc.sync.dma_start(out=cash_bf[:], in_=cash.rearrange("(g p t) -> p g t", p=P, t=4))
         nc.sync.dma_start(out=disc_rows[0 : S // P, :], in_=discount.rearrange("(j c) -> j c", c=P))
-        for k in range(TG):
-            load_n(n_raw12[:, k, :, :], k, KP, N)
-        nc.sync.dma_start(out=disc_row[:], in_=discount.partition_broadcast(P))
+        for g in range(1, NG):
+            for k in range(TG):
+                load_n(n_raw12[:, g - 1, k, :, :], k, KP * g, KP * (g + 1))
+            if g == 1:
+                nc.sync.dma_start(out=disc_row[:], in_=discount.partition_broadcast(P))
 
         def permute_w(k0, k1):
             nc.vector.tensor_copy(
@@ -153,6 +155,7 @@ def tile_shock_floor_netting_hedge_h2_kernel(
             turned = bank("b")
             for t in range(4):
                 nc.tensor.transpose(turned[:, P * t : P * (t + 1)], rows_f32[:, t, :], ident[:])
+            group_n_quarter(0, 0, 0, 4)
             nc.scalar.copy(out=cols[:], in_=turned[:].rearrange("p (t c) -> p t c", t=4)[:, :, 0:TG])
 
         def turn_discount():
@@ -216,7 +219,7 @@ def tile_shock_floor_netting_hedge_h2_kernel(
         def n_views(g, h):
             if ("n", g, h) not in staged:
                 staged["n", g, h] = rotating("grouped", 4, [P, 2, KP, 4], BF16)
-            raw = n_raw0[h][:] if g == 0 else n_raw12[:, 2 * h : 2 * h + 2, :, KP * (g - 1) : KP * g]
+            raw = n_raw0[h][:] if g == 0 else n_raw12[:, g - 1, 2 * h : 2 * h + 2, :, :]
             dst = staged["n", g, h][:].rearrange("p k (u m) t -> p k m u t", u=4)
             src = raw.rearrange("p k t (m u) -> p k m u t", u=4)
             return dst, src
@@ -229,9 +232,9 @@ def tile_shock_floor_netting_hedge_h2_kernel(
             dst, src = n_views(g, k // 2)
             nc.vector.tensor_copy(out=dst[:, k % 2, :, :, :], in_=src[:, k % 2, :, :, :])
 
-        def group_n_quarter(g, k, quarter):
+        def group_n_quarter(g, k, quarter, count=1):
             dst, src = n_views(g, k // 2)
-            m = slice(32 * quarter, 32 * (quarter + 1))
+            m = slice(32 * quarter, 32 * (quarter + count))
             nc.scalar.copy(out=dst[:, k % 2, m, :, :], in_=src[:, k % 2, m, :, :])
 
         def quantize_n(g, h):
@@ -338,38 +341,36 @@ def tile_shock_floor_netting_hedge_h2_kernel(
                     in_=y_plane[32 * q : 32 * q + 4, g0:g1, :].bitcast(I32),
                 )
 
-        for quarter in range(4):
-            group_n_quarter(0, 0, quarter)
         turn_vectors()
-        permute_w(0, 1)
         permute_w_plane()
+        permute_w(0, 1)
         stage1(0, 0)
-        permute_w(1, 2)
-        stage1(0, 1)
         group_n(0, 1)
-        permute_w(2, 4)
+        permute_w(1, 2)
         quantize_n(0, 0)
         group_n(0, 2)
-        stage1(0, 2)
-        group_v(0, 0)
+        permute_w(2, 4)
         group_n(0, 3)
+        hedge_columns()
+        stage1(0, 1)
+        group_v(0, 0)
+        quantize_n(0, 1)
         quantize_v(0, 0)
+        stage1(0, 2)
         stage1(0, 3)
         group_v(0, 1)
-        quantize_n(0, 1)
-        hedge_columns()
+        group_n(1, 0)
         quantize_v(0, 1)
-        for k in range(TG):
-            stage1(1, k)
+        stage1(1, 0)
+        stage1(1, 1)
         group_v(1, 0)
+        stage1(1, 2)
+        stage1(1, 3)
         group_v(1, 1)
         quantize_v(1, 0)
         quantize_v(1, 1)
 
-        scalar_quarters = {
-            (0, 0): [(1, 0, 0)], (0, 1): [(1, 0, 1)], (0, 2): [(1, 0, 2)], (0, 3): [(1, 0, 3)],
-            (1, 1): [(2, 0, 0)], (1, 2): [(2, 0, 1)], (1, 3): [(2, 0, 2), (2, 0, 3)],
-        }
+        scalar_quarters = {(0, 0): [(1, 1, 0)], (0, 1): [(1, 1, 1)], (0, 2): [(1, 1, 2)], (0, 3): [(1, 1, 3)]}
 
         def unit(u):
             for t in range(4):
@@ -383,32 +384,29 @@ def tile_shock_floor_netting_hedge_h2_kernel(
 
         unit(0)
         group_n_pair(1, 1)
-        group_n(1, 1)
-        quantize_n(1, 1)
         quantize_n(1, 0)
-        unit(1)
-        group_n_pair(2, 1)
+        quantize_n(1, 1)
         group_y(0)
-        group_n(2, 1)
-        quantize_n(2, 1)
+        group_n_pair(2, 0)
+        group_n_pair(2, 1)
         quantize_n(2, 0)
+        quantize_n(2, 1)
         quantize_y(0)
+        unit(1)
         unit(2)
-        store_words(0)
-        group_y(1)
         group_y(2)
+        group_y(1)
+        quantize_y(2)
         quantize_y(1)
         unit(3)
+        store_words(0)
         group_y(3)
-        quantize_y(2)
-        store_words(1)
         unit(4)
         store_words(2)
-        quantize_y(3)
+        store_words(1)
         group_y(4)
+        quantize_y(3)
         quantize_y(4)
-        store_words(3)
-        store_scales(0, 2, [nc.sync])
         stage2(5, 0)
         turn(4)
         discount_tile(4, 0)
@@ -418,6 +416,8 @@ def tile_shock_floor_netting_hedge_h2_kernel(
         stage2(5, 1)
         discount_tile(4, 3)
         store_rows(4, 2, 4, nc.sync)
+        store_words(3)
+        store_scales(0, 2, [nc.sync])
         stage2(5, 2)
         stage2(5, 3)
         store_words(4)

@@ -27,6 +27,13 @@ QUANTIZE_WORDS = {1024: (1024,), 768: (512, 256), 512: (512,), 384: (256, 128), 
 STAGE2_WIDTHS = {512: (512,), 384: (256, 128), 256: (256,), 128: (128,)}
 
 
+BANKS = {"a": 3, "b": 4}
+SLOT = {("n", 0, 0): 0, ("n", 0, 1): 1, ("v", 0, 0): 2, ("v", 0, 1): 0, ("n", 1, 0): 1, ("n", 1, 1): 2, ("v", 1, 0): 0,
+        ("v", 1, 1): 3, ("n", 2, 0): 0, ("n", 2, 1): 1,
+        ("y", 0): 3, ("y", 1): 3, ("y", 2): 2, ("y", 3): 2, ("y", 4): 3, ("y", 5): 3, ("y", 6): 0}
+POOL_SHARE = 4
+
+
 def windows(widths):
     out = []
     c = 0
@@ -43,7 +50,7 @@ def tile_shock_floor_netting_hedge_h2_kernel(
     with ExitStack() as ctx:
         keep = ctx.enter_context(tc.tile_pool(name="keep", bufs=1))
         work = ctx.enter_context(tc.tile_pool(name="work", bufs=2))
-        psum = ctx.enter_context(tc.psum_pool(name="psum", bufs=4))
+        psum = ctx.enter_context(tc.psum_pool(name="psum", bufs=1))
         ctx.enter_context(tc.manual_schedule())
 
         def kept(name, shape, dtype):
@@ -53,12 +60,15 @@ def tile_shock_floor_netting_hedge_h2_kernel(
             return work.tile(shape, dtype, name=tag, tag=tag, bufs=bufs, align_bytes=64)
 
         def bank(tag):
-            return psum.tile([P, 512], F32, name=tag, tag=tag)
+            return psum.tile([P, 512], F32, name=tag, tag=tag, bufs=BANKS[tag])
+
+        def staging(slot, shape, dtype):
+            return rotating("staging%d" % slot, 1, shape, dtype)
 
         x_codes = [kept("x_codes%d" % c, [P, RG, CHUNKS[c][1]], U32) for c in range(2)]
         x_plane = kept("x_plane", [P, RG, S], U8)
         w_raw = rotating("y", 2, [P, TG, RG, 256], I32)
-        w_plane_raw = rotating("y_bf", 2, [P, RG, T], U8)
+        w_plane_raw = staging(3, [P, RG, T], U8)
         w_codes = kept("w_codes", [P, TG, RG, 1024], U8)
         w_plane = kept("w_plane", [P, RG, T], U8)
         n_raw0 = [rotating("z_wide", 2, [P, 2, 4, KP], BF16) for half in range(2)]
@@ -72,7 +82,9 @@ def tile_shock_floor_netting_hedge_h2_kernel(
         rows_f32 = rotating("y_last", 1, [P, 4, P], F32)
         cols = kept("cols", [P, 4, TG], F32)
         disc_rows = kept("disc_rows", [P, P], BF16)
-        disc_rows_f32 = kept("disc_rows_f32", [P, P], F32)
+        ident_bf = kept("ident_bf", [P, P], BF16)
+        disc_col_bf = kept("disc_col_bf", [P, 8], BF16)
+        disc_bank = psum.tile([P, 1024], BF16, name="disc_bank")
         disc_col = kept("disc_col", [P, 8], F32)
         ident = kept("ident", [P, P], F32)
         hedge_bf = kept("hedge_bf", [P, NG, 4], BF16)
@@ -80,12 +92,9 @@ def tile_shock_floor_netting_hedge_h2_kernel(
         hedge_col = kept("hedge_col", [P, NG, 4], F32)
         cash_hedge = kept("cash_hedge", [P, NG, 4], F32)
         disc_row = kept("disc_row", [P, S], BF16)
-        warm = kept("warm", [P, 2], F32)
 
         nc.vector.memset(rows[:], 0.0)
-        nc.vector.memset(warm[:, 0:1], 0.0)
         nc.scalar.dma_start(out=rows[0:TG, :], in_=base_value.rearrange("(k c) -> k c", k=TG))
-        nc.scalar.activation(out=warm[:, 1:2], in_=warm[:, 0:1], func=ACT.Relu)
         nc.vector.memset(w_plane_raw[:].rearrange("p g c -> p (g c)").bitcast(I32), 0)
         nc.vector.memset(x_plane[:].rearrange("p g c -> p (g c)").bitcast(I32), 0)
 
@@ -116,6 +125,7 @@ def tile_shock_floor_netting_hedge_h2_kernel(
         load_x(0, nc.gpsimd)
         load_w(0, nc.gpsimd)
         make_identity(nc, ident[:])
+        nc.scalar.copy(out=ident_bf[:], in_=ident[:])
         nc.gpsimd.memset(disc_rows[:], 0.0)
         load_plane(w_plane_raw, w_scales)
         load_plane(x_plane, x_scales)
@@ -159,12 +169,17 @@ def tile_shock_floor_netting_hedge_h2_kernel(
             nc.scalar.copy(out=cols[:], in_=turned[:].rearrange("p (t c) -> p t c", t=4)[:, :, 0:TG])
 
         def turn_discount():
-            turned = bank("a")
-            nc.tensor.transpose(turned[:, 0:P], disc_rows_f32[:], ident[:])
-            nc.scalar.copy(out=disc_col[:], in_=turned[:, 0:8])
+            nc.tensor.transpose(disc_bank[:, S : S + P], disc_rows[:], ident_bf[:])
+            nc.scalar.copy(out=disc_col[:], in_=disc_bank[:, S : S + 8])
+            nc.scalar.copy(out=disc_col_bf[:], in_=disc_bank[:, S : S + 8])
+
+        def spread_discount():
+            for j in range(S // P):
+                nc.tensor.transpose(
+                    disc_bank[:, P * j : P * (j + 1)], disc_col_bf[:, j : j + 1].to_broadcast([P, P]), ident_bf[:]
+                )
 
         def hedge_columns():
-            nc.vector.tensor_copy(out=disc_rows_f32[:], in_=disc_rows[:])
             nc.vector.tensor_copy(out=hedge_col[:], in_=hedge_bf[:])
             nc.vector.tensor_tensor(out=cash_hedge[:], in0=cash_bf[:], in1=hedge_bf[:], op=ALU.mult)
 
@@ -201,12 +216,13 @@ def tile_shock_floor_netting_hedge_h2_kernel(
                     in_=grouped[:, 4 * c0 : 4 * (c0 + w)],
                 )
 
-        def group_v(c, h):
+        def group_v(c, h, k0=0, k1=2):
             width = CHUNKS[c][1]
-            staged["v", c, h] = rotating("grouped", 4, [P, 2, width, 4], BF16)
+            if k0 == 0:
+                staged["v", c, h] = staging(SLOT["v", c, h], [P, 2, width, 4], BF16)
             nc.vector.tensor_copy(
-                out=staged["v", c, h][:].rearrange("p k (a i) t -> p k a t i", i=4),
-                in_=v_rows[c, h][:].rearrange("p k t (a i) -> p k a t i", i=4),
+                out=staged["v", c, h][:, k0:k1, :, :].rearrange("p k (a i) t -> p k a t i", i=4),
+                in_=v_rows[c, h][:, k0:k1, :, :].rearrange("p k t (a i) -> p k a t i", i=4),
             )
 
         def quantize_v(c, h):
@@ -218,7 +234,7 @@ def tile_shock_floor_netting_hedge_h2_kernel(
 
         def n_views(g, h):
             if ("n", g, h) not in staged:
-                staged["n", g, h] = rotating("grouped", 4, [P, 2, KP, 4], BF16)
+                staged["n", g, h] = staging(SLOT["n", g, h], [P, 2, KP, 4], BF16)
             raw = n_raw0[h][:] if g == 0 else n_raw12[:, g - 1, 2 * h : 2 * h + 2, :, :]
             dst = staged["n", g, h][:].rearrange("p k (u m) t -> p k m u t", u=4)
             src = raw.rearrange("p k t (m u) -> p k m u t", u=4)
@@ -244,7 +260,7 @@ def tile_shock_floor_netting_hedge_h2_kernel(
                 staged["n", g, h][:].rearrange("p k n t -> p (k n t)"),
             )
 
-        units = [(0, 0, 512), (0, 512, 384), (1, 0, 512), (1, 512, 384), (2, 0, 512), (2, 512, 256), (2, 768, 128)]
+        units = [(0, 0, 512), (1, 0, 512), (0, 512, 384), (1, 512, 384), (2, 0, 512), (2, 512, 256), (2, 768, 128)]
         z = {}
         y_words = {}
 
@@ -277,9 +293,8 @@ def tile_shock_floor_netting_hedge_h2_kernel(
         turned_z = {}
         y_rows = {}
 
-        def turn(u):
-            width = units[u][2]
-            for j in range(width // P):
+        def turn(u, j0, j1):
+            for j in range(j0, j1):
                 turned_z[u, j] = bank("b")
                 for t in range(4):
                     nc.tensor.transpose(turned_z[u, j][:, P * t : P * (t + 1)], z[u][:, t, P * j : P * (j + 1)], ident[:])
@@ -307,29 +322,39 @@ def tile_shock_floor_netting_hedge_h2_kernel(
 
         def turn_and_store(u):
             tiles = units[u][2] // P
-            turn(u)
             for j in range(tiles):
+                turn(u, j, j + 1)
                 discount_tile(u, j)
                 if j % 2 == 1 or j == tiles - 1:
                     store_rows(u, j - j % 2, j + 1, nc.sync)
 
         def group_y(u):
             g, s0, width = units[u]
-            staged["y", u] = rotating("y_bf", 2, [P, width, 4], BF16)
+            staged["y", u] = staging(SLOT["y", u], [P, width, 4], BF16)
+            cut = width - width // POOL_SHARE
+            nc.gpsimd.tensor_tensor(
+                out=staged["y", u][:, cut:width, :],
+                in0=z[u][:, :, cut:width].rearrange("p t s -> p s t"),
+                in1=disc_row[:, s0 + cut : s0 + width].unsqueeze(2).to_broadcast([P, width - cut, 4]),
+                op=ALU.mult,
+            )
             nc.vector.tensor_tensor(
-                out=staged["y", u][:].rearrange("p (a i) t -> p a t i", i=4),
-                in0=z[u][:].rearrange("p t (a i) -> p a t i", i=4),
-                in1=disc_row[:, s0 : s0 + width].rearrange("p (a i) -> p a i", i=4).unsqueeze(2).to_broadcast([P, width // 4, 4, 4]),
+                out=staged["y", u][:, 0:cut, :].rearrange("p (a i) t -> p a t i", i=4),
+                in0=z[u][:, :, 0:cut].rearrange("p t (a i) -> p a t i", i=4),
+                in1=disc_bank[:, s0 : s0 + cut].rearrange("p (a i) -> p a i", i=4).unsqueeze(2).to_broadcast([P, cut // 4, 4, 4]),
                 op=ALU.mult,
             )
 
         def quantize_y(u):
             g, s0, width = units[u]
-            y_words[u] = rotating("y_words", 4, [P, width], U32)
-            quantize(y_words[u][:], y_plane[:, g, s0 : s0 + width], staged["y", u][:].rearrange("p s t -> p (s t)"))
+            if u != 6:
+                y_words[u] = rotating("y_words", 4, [P, 384 if u == 5 else width], U32)
+            words = y_words[5][:, 256:384] if u == 6 else y_words[u][:, 0:width]
+            quantize(words, y_plane[:, g, s0 : s0 + width], staged["y", u][:].rearrange("p s t -> p (s t)"))
 
         def store_words(u):
             g, s0, width = units[u]
+            width = y_words[u].shape[1]
             nc.sync.dma_start(
                 out=out_1[g].rearrange("p s t -> p (s t)").bitcast(I32)[:, s0 : s0 + width], in_=y_words[u][:].bitcast(I32)
             )
@@ -337,8 +362,8 @@ def tile_shock_floor_netting_hedge_h2_kernel(
         def store_scales(g0, g1, queues):
             for q in range(4):
                 queues[q % len(queues)].dma_start(
-                    out=out_2[g0:g1, 4 * q : 4 * q + 4, :].rearrange("g r s -> r g s").bitcast(I32),
-                    in_=y_plane[32 * q : 32 * q + 4, g0:g1, :].bitcast(I32),
+                    out=out_2[g0:g1, q:16:4, :].rearrange("g r s -> r g s").bitcast(I32),
+                    in_=y_plane[q:P:32, g0:g1, :].bitcast(I32),
                 )
 
         turn_vectors()
@@ -346,10 +371,10 @@ def tile_shock_floor_netting_hedge_h2_kernel(
         permute_w(0, 1)
         stage1(0, 0)
         group_n(0, 1)
-        permute_w(1, 2)
+        permute_w(1, 3)
         quantize_n(0, 0)
         group_n(0, 2)
-        permute_w(2, 4)
+        permute_w(3, 4)
         group_n(0, 3)
         hedge_columns()
         stage1(0, 1)
@@ -361,31 +386,32 @@ def tile_shock_floor_netting_hedge_h2_kernel(
         group_v(0, 1)
         group_n(1, 0)
         quantize_v(0, 1)
-        stage1(1, 0)
-        stage1(1, 1)
-        group_v(1, 0)
-        stage1(1, 2)
-        stage1(1, 3)
-        group_v(1, 1)
-        quantize_v(1, 0)
-        quantize_v(1, 1)
+        for k in range(TG):
+            stage1(1, k)
 
-        scalar_quarters = {(0, 0): [(1, 1, 0)], (0, 1): [(1, 1, 1)], (0, 2): [(1, 1, 2)], (0, 3): [(1, 1, 3)]}
+        scalar_quarters = {}
 
         def unit(u):
             for t in range(4):
                 stage2(u, t)
-                if (u, t) == (1, 0):
+                if (u, t) == (0, 0):
                     turn_discount()
+                if (u, t) == (0, 2):
+                    spread_discount()
                 if t == 0 and 0 < u < 5:
                     turn_and_store(u - 1)
                 for g, k, quarter in scalar_quarters.get((u, t), []):
                     group_n_quarter(g, k, quarter)
 
-        unit(0)
+        group_n(1, 1)
         group_n_pair(1, 1)
+        unit(0)
         quantize_n(1, 0)
         quantize_n(1, 1)
+        group_v(1, 0)
+        group_v(1, 1)
+        quantize_v(1, 0)
+        quantize_v(1, 1)
         group_y(0)
         group_n_pair(2, 0)
         group_n_pair(2, 1)
@@ -394,22 +420,23 @@ def tile_shock_floor_netting_hedge_h2_kernel(
         quantize_y(0)
         unit(1)
         unit(2)
-        group_y(2)
         group_y(1)
-        quantize_y(2)
+        group_y(2)
         quantize_y(1)
+        quantize_y(2)
         unit(3)
         store_words(0)
         group_y(3)
         unit(4)
-        store_words(2)
         store_words(1)
+        store_words(2)
         group_y(4)
         quantize_y(3)
         quantize_y(4)
         stage2(5, 0)
-        turn(4)
+        turn(4, 0, 3)
         discount_tile(4, 0)
+        turn(4, 3, 4)
         discount_tile(4, 1)
         store_rows(4, 0, 2, nc.sync)
         discount_tile(4, 2)
@@ -417,7 +444,6 @@ def tile_shock_floor_netting_hedge_h2_kernel(
         discount_tile(4, 3)
         store_rows(4, 2, 4, nc.sync)
         store_words(3)
-        store_scales(0, 2, [nc.sync])
         stage2(5, 2)
         stage2(5, 3)
         store_words(4)
@@ -426,17 +452,16 @@ def tile_shock_floor_netting_hedge_h2_kernel(
         stage2(6, 1)
         stage2(6, 2)
         stage2(6, 3)
-        turn(5)
-        turn(6)
+        turn(5, 0, 2)
+        turn(6, 0, 1)
         group_y(6)
         quantize_y(5)
         quantize_y(6)
         discount_tile(5, 0)
         store_rows(5, 0, 1, nc.sync)
         discount_tile(5, 1)
+        store_rows(5, 1, 2, nc.sync)
         discount_tile(6, 0)
         store_words(5)
-        store_rows(5, 1, 2, nc.sync)
         store_rows(6, 0, 1, nc.scalar)
-        store_words(6)
-        store_scales(2, 3, [nc.sync, nc.scalar])
+        store_scales(0, 3, [nc.sync, nc.scalar])

from contextlib import ExitStack

import concourse.mybir as mybir
from concourse.masks import make_identity

S, R, T, N = 896, 1024, 2048, 1536
FLOPS = 2 * S * R * T + 2 * S * T * N

F32 = mybir.dt.float32
BF16 = mybir.dt.bfloat16
I32 = mybir.dt.int32
U32 = mybir.dt.uint32
U8 = mybir.dt.uint8
FP8X4 = mybir.dt.float8_e4m3fn_x4
FP4X4 = mybir.dt.float4_e2m1fn_x4
ACT = mybir.ActivationFunctionType
ALU = mybir.AluOpType

P = 128
KP = 512
RG = R // KP
TG = T // KP
NG = N // KP
CHUNKS = ((0, 512), (512, 384))
STAGE1_WIDTHS = {512: (512,), 384: (128, 128, 128)}
QUANTIZE_WORDS = {1024: (1024,), 768: (512, 256), 512: (512,), 384: (256, 128), 256: (256,), 128: (128,)}
STAGE2_WIDTHS = {512: (512,), 384: (256, 128), 256: (256,), 128: (128,)}


BANKS = {"a": 3, "b": 4}
SLOT = {("n", 0, 0): 0, ("n", 0, 1): 1, ("v", 0, 0): 2, ("v", 0, 1): 0, ("n", 1, 0): 1, ("n", 1, 1): 2, ("v", 1, 0): 0,
        ("v", 1, 1): 3, ("n", 2, 0): 0, ("n", 2, 1): 1,
        ("y", 0): 3, ("y", 1): 3, ("y", 2): 2, ("y", 3): 2, ("y", 4): 3, ("y", 5): 3, ("y", 6): 0}
POOL_SHARE = 4


def windows(widths):
    out = []
    c = 0
    for w in widths:
        out.append((c, w))
        c += w
    return out


def tile_shock_floor_netting_hedge_h2_kernel(
    tc, x_words, x_scales, w_words, w_scales, base_value, netting, cash, discount, hedge_ratio, out_0, out_1, out_2
):
    nc = tc.nc
    with ExitStack() as ctx:
        keep = ctx.enter_context(tc.tile_pool(name="keep", bufs=1))
        work = ctx.enter_context(tc.tile_pool(name="work", bufs=2))
        psum = ctx.enter_context(tc.psum_pool(name="psum", bufs=1))
        ctx.enter_context(tc.manual_schedule())

        def kept(name, shape, dtype):
            return keep.tile(shape, dtype, name=name, align_bytes=64)

        def rotating(tag, bufs, shape, dtype):
            return work.tile(shape, dtype, name=tag, tag=tag, bufs=bufs, align_bytes=64)

        def bank(tag):
            return psum.tile([P, 512], F32, name=tag, tag=tag, bufs=BANKS[tag])

        def staging(slot, shape, dtype):
            return rotating("staging%d" % slot, 1, shape, dtype)

        x_codes = [kept("x_codes%d" % c, [P, RG, CHUNKS[c][1]], U32) for c in range(2)]
        x_plane = kept("x_plane", [P, RG, S], U8)
        w_raw = rotating("y", 2, [P, TG, RG, 256], I32)
        w_plane_raw = staging(3, [P, RG, T], U8)
        w_codes = kept("w_codes", [P, TG, RG, 1024], U8)
        w_plane = kept("w_plane", [P, RG, T], U8)
        n_raw0 = [rotating("z_wide", 2, [P, 2, 4, KP], BF16) for half in range(2)]
        n_raw12 = kept("n_raw12", [P, NG - 1, TG, 4, KP], BF16)
        n_codes = kept("n_codes", [P, NG, TG, KP], U32)
        n_plane = kept("n_plane", [P, NG, TG, KP], U8)
        v_codes = [kept("v_codes%d" % c, [P, TG, CHUNKS[c][1]], U32) for c in range(2)]
        v_plane = [kept("v_plane%d" % c, [P, TG, CHUNKS[c][1]], U8) for c in range(2)]
        y_plane = kept("y_plane", [P, NG, S], U8)
        rows = kept("rows", [P, KP], BF16)
        rows_f32 = rotating("y_last", 1, [P, 4, P], F32)
        cols = kept("cols", [P, 4, TG], F32)
        disc_rows = kept("disc_rows", [P, P], BF16)
        ident_bf = kept("ident_bf", [P, P], BF16)
        disc_col_bf = kept("disc_col_bf", [P, 8], BF16)
        disc_bank = psum.tile([P, 1024], BF16, name="disc_bank")
        disc_col = kept("disc_col", [P, 8], F32)
        ident = kept("ident", [P, P], F32)
        hedge_bf = kept("hedge_bf", [P, NG, 4], BF16)
        cash_bf = kept("cash_bf", [P, NG, 4], BF16)
        hedge_col = kept("hedge_col", [P, NG, 4], F32)
        cash_hedge = kept("cash_hedge", [P, NG, 4], F32)
        disc_row = kept("disc_row", [P, S], BF16)

        nc.vector.memset(rows[:], 0.0)
        nc.scalar.dma_start(out=rows[0:TG, :], in_=base_value.rearrange("(k c) -> k c", k=TG))
        nc.vector.memset(w_plane_raw[:].rearrange("p g c -> p (g c)").bitcast(I32), 0)
        nc.vector.memset(x_plane[:].rearrange("p g c -> p (g c)").bitcast(I32), 0)


        w_src = w_words.rearrange("g p c -> p g c").bitcast(I32)
        x_src = x_words.rearrange("g p n t -> p g (n t)").bitcast(I32)
        n_src = netting.rearrange("(k q t r) n -> k t q r n", q=16, t=4, r=8)

        def load_w(k, queue):
            queue.dma_start(out=w_raw[:, k, :, :], in_=w_src[:, :, 256 * k : 256 * (k + 1)])

        def load_x(c, queue):
            s0, width = CHUNKS[c]
            queue.dma_start(out=x_codes[c][:].bitcast(I32), in_=x_src[:, :, s0 : s0 + width])

        def load_plane(plane, scales):
            for r in range(4):
                nc.sync.dma_start(
                    out=plane[r:P:32, :, :].bitcast(I32),
                    in_=scales[:, r:16:4, :].rearrange("g q c -> q g c").bitcast(I32),
                )

        def load_n(raw, k, n0, n1):
            for t in range(4):
                nc.sync.dma_start(out=raw[:, t, :], in_=n_src[k, t, :, :, n0:n1])

        load_n(n_raw0[0][:, 0, :, :], 0, 0, KP)
        load_x(0, nc.gpsimd)
        load_w(0, nc.gpsimd)
        make_identity(nc, ident[:])
        nc.scalar.copy(out=ident_bf[:], in_=ident[:])
        nc.gpsimd.memset(disc_rows[:], 0.0)
        load_plane(w_plane_raw, w_scales)
        load_plane(x_plane, x_scales)
        load_n(n_raw0[0][:, 1, :, :], 1, 0, KP)
        load_w(1, nc.sync)
        load_w(2, nc.sync)
        load_n(n_raw0[1][:, 0, :, :], 2, 0, KP)
        load_w(3, nc.sync)
        load_n(n_raw0[1][:, 1, :, :], 3, 0, KP)
        load_x(1, nc.sync)
        nc.sync.dma_start(out=hedge_bf[:], in_=hedge_ratio.rearrange("(g p t) -> p g t", p=P, t=4))
        nc.sync.dma_start(out=cash_bf[:], in_=cash.rearrange("(g p t) -> p g t", p=P, t=4))
        nc.sync.dma_start(out=disc_rows[0 : S // P, :], in_=discount.rearrange("(j c) -> j c", c=P))
        for g in range(1, NG):
            for k in range(TG):
                load_n(n_raw12[:, g - 1, k, :, :], k, KP * g, KP * (g + 1))
            if g == 1:
                nc.sync.dma_start(out=disc_row[:], in_=discount.partition_broadcast(P))

        def permute_w(k0, k1):
            nc.vector.tensor_copy(
                out=w_codes[:, k0:k1, :, :].bitcast(I32).rearrange("p k g (t q w) -> p (k g) t q w", t=4, w=4),
                in_=w_raw[:, k0:k1, :, :].rearrange("p k g (q t w) -> p (k g) t q w", t=4, w=4),
            )

        def permute_w_plane():
            nc.vector.tensor_copy(
                out=w_plane[:].rearrange("p g c -> p (g c)").bitcast(I32).rearrange("p (k t q w) -> p k t q w", t=4, q=16, w=2),
                in_=w_plane_raw[:].rearrange("p g c -> p (g c)").bitcast(I32).rearrange("p (k q t w) -> p k t q w", t=4, q=16, w=2),
            )

        def turn_vectors():
            nc.vector.tensor_copy(
                out=rows_f32[:].rearrange("p t (q r) -> p t q r", r=8),
                in_=rows[:].rearrange("p (q t r) -> p t q r", t=4, r=8),
            )
            turned = bank("b")
            for t in range(4):
                nc.tensor.transpose(turned[:, P * t : P * (t + 1)], rows_f32[:, t, :], ident[:])
            group_n_quarter(0, 0, 0, 4)
            nc.scalar.copy(out=cols[:], in_=turned[:].rearrange("p (t c) -> p t c", t=4)[:, :, 0:TG])

        def turn_discount():
            nc.tensor.transpose(disc_bank[:, S : S + P], disc_rows[:], ident_bf[:])
            nc.scalar.copy(out=disc_col[:], in_=disc_bank[:, S : S + 8])
            nc.scalar.copy(out=disc_col_bf[:], in_=disc_bank[:, S : S + 8])

        def spread_discount():
            for j in range(S // P):
                nc.tensor.transpose(
                    disc_bank[:, P * j : P * (j + 1)], disc_col_bf[:, j : j + 1].to_broadcast([P, P]), ident_bf[:]
                )

        def hedge_columns():
            nc.vector.tensor_copy(out=hedge_col[:], in_=hedge_bf[:])
            nc.vector.tensor_tensor(out=cash_hedge[:], in0=cash_bf[:], in1=hedge_bf[:], op=ALU.mult)

        v_rows = {}
        staged = {}

        def stage1(c, k):
            s0, width = CHUNKS[c]
            if k % 2 == 0:
                v_rows[c, k // 2] = rotating("v_rows%d" % c, 2, [P, 2, 4, width], BF16)
            for t in range(4):
                acc = bank("ab"[t % 2])
                col = 4 * k + t
                for c0, w in windows(STAGE1_WIDTHS[width]):
                    for g in range(RG):
                        nc.tensor.matmul_mx(
                            out=acc[:, c0 : c0 + w],
                            lhsT=w_codes[:, k, g, 256 * t : 256 * (t + 1)].bitcast(FP4X4),
                            lhsT_scale=w_plane[:, g, P * col : P * (col + 1)],
                            rhs=x_codes[c][:, g, c0 : c0 + w].bitcast(FP8X4),
                            rhs_scale=x_plane[:, g, s0 + c0 : s0 + c0 + w],
                            start=(g == 0),
                            stop=(g == RG - 1),
                        )
                nc.scalar.activation(
                    out=v_rows[c, k // 2][:, k % 2, t, :], in_=acc[:, 0:width], func=ACT.Relu, bias=cols[:, t, k : k + 1]
                )

        def quantize(words, plane, grouped):
            for c0, w in windows(QUANTIZE_WORDS[words.shape[1]]):
                nc.vector.quantize_mx(
                    out=words[:, c0 : c0 + w].bitcast(FP8X4),
                    scales=plane[:, c0 : c0 + w],
                    in_=grouped[:, 4 * c0 : 4 * (c0 + w)],
                )

        def group_v(c, h, k0=0, k1=2):
            width = CHUNKS[c][1]
            if k0 == 0:
                staged["v", c, h] = staging(SLOT["v", c, h], [P, 2, width, 4], BF16)
            nc.vector.tensor_copy(
                out=staged["v", c, h][:, k0:k1, :, :].rearrange("p k (a i) t -> p k a t i", i=4),
                in_=v_rows[c, h][:, k0:k1, :, :].rearrange("p k t (a i) -> p k a t i", i=4),
            )

        def quantize_v(c, h):
            quantize(
                v_codes[c][:, 2 * h : 2 * h + 2, :].rearrange("p k s -> p (k s)"),
                v_plane[c][:, 2 * h : 2 * h + 2, :].rearrange("p k s -> p (k s)"),
                staged["v", c, h][:].rearrange("p k s t -> p (k s t)"),
            )

        def n_views(g, h):
            if ("n", g, h) not in staged:
                staged["n", g, h] = staging(SLOT["n", g, h], [P, 2, KP, 4], BF16)
            raw = n_raw0[h][:] if g == 0 else n_raw12[:, g - 1, 2 * h : 2 * h + 2, :, :]
            dst = staged["n", g, h][:].rearrange("p k (u m) t -> p k m u t", u=4)
            src = raw.rearrange("p k t (m u) -> p k m u t", u=4)
            return dst, src

        def group_n_pair(g, h):
            dst, src = n_views(g, h)
            nc.vector.tensor_copy(out=dst, in_=src)

        def group_n(g, k):
            dst, src = n_views(g, k // 2)
            nc.vector.tensor_copy(out=dst[:, k % 2, :, :, :], in_=src[:, k % 2, :, :, :])

        def group_n_quarter(g, k, quarter, count=1):
            dst, src = n_views(g, k // 2)
            m = slice(32 * quarter, 32 * (quarter + count))
            nc.scalar.copy(out=dst[:, k % 2, m, :, :], in_=src[:, k % 2, m, :, :])

        def quantize_n(g, h):
            quantize(
                n_codes[:, g, 2 * h : 2 * h + 2, :].rearrange("p k n -> p (k n)"),
                n_plane[:, g, 2 * h : 2 * h + 2, :].rearrange("p k n -> p (k n)"),
                staged["n", g, h][:].rearrange("p k n t -> p (k n t)"),
            )

        units = [(0, 0, 512), (1, 0, 512), (0, 512, 384), (1, 512, 384), (2, 0, 512), (2, 512, 256), (2, 768, 128)]
        z = {}
        y_words = {}

        def stage2(u, t):
            g, s0, width = units[u]
            if t == 0:
                z[u] = rotating({512: "z_wide", 128: "z_last"}.get(width, "z_narrow"), 1 if width == P else 2, [P, 4, width], F32)
            acc = bank("a")
            c = s0 // KP
            c1 = s0 - CHUNKS[c][0]
            for c0, w in windows(STAGE2_WIDTHS[width]):
                for k in range(TG):
                    nc.tensor.matmul_mx(
                        out=acc[:, c0 : c0 + w],
                        lhsT=n_codes[:, g, k, P * t : P * (t + 1)].bitcast(FP8X4),
                        lhsT_scale=n_plane[:, g, k, P * t : P * (t + 1)],
                        rhs=v_codes[c][:, k, c1 + c0 : c1 + c0 + w].bitcast(FP8X4),
                        rhs_scale=v_plane[c][:, k, c1 + c0 : c1 + c0 + w],
                        start=(k == 0),
                        stop=(k == TG - 1),
                    )
            nc.scalar.activation(
                out=z[u][:, t, :],
                in_=acc[:, 0:width],
                func=ACT.Identity,
                scale=hedge_col[:, g, t : t + 1],
                bias=cash_hedge[:, g, t : t + 1],
            )

        turned_z = {}
        y_rows = {}

        def turn(u, j0, j1):
            for j in range(j0, j1):
                turned_z[u, j] = bank("b")
                for t in range(4):
                    nc.tensor.transpose(turned_z[u, j][:, P * t : P * (t + 1)], z[u][:, t, P * j : P * (j + 1)], ident[:])

        def discount_tile(u, j, on_vector=False):
            g, s0, width = units[u]
            if j == 0:
                y_rows[u] = rotating("y" if width > P else "y_last", 2 if width > P else 1, [P, width // P, KP], F32)
            natural = y_rows[u][:, j, :].rearrange("s (p t) -> s p t", t=4)
            by_slot = turned_z[u, j][:].rearrange("s (t p) -> s p t", t=4)
            row = s0 // P + j
            if on_vector:
                nc.vector.tensor_scalar(
                    out=natural, in0=by_slot, scalar1=disc_col[:, row : row + 1], scalar2=None, op0=ALU.mult
                )
            else:
                nc.scalar.activation(out=natural, in_=by_slot, func=ACT.Copy, scale=disc_col[:, row : row + 1])

        def store_rows(u, j0, j1, queue):
            g, s0, width = units[u]
            queue.dma_start(
                out=out_0[s0 + P * j0 : s0 + P * j1, KP * g : KP * (g + 1)].rearrange("(j s) n -> s j n", s=P),
                in_=y_rows[u][:, j0:j1, :],
            )

        def turn_and_store(u):
            tiles = units[u][2] // P
            for j in range(tiles):
                turn(u, j, j + 1)
                discount_tile(u, j)
                if j % 2 == 1 or j == tiles - 1:
                    store_rows(u, j - j % 2, j + 1, nc.sync)

        def group_y(u):
            g, s0, width = units[u]
            staged["y", u] = staging(SLOT["y", u], [P, width, 4], BF16)
            cut = width - width // POOL_SHARE
            nc.gpsimd.tensor_tensor(
                out=staged["y", u][:, cut:width, :],
                in0=z[u][:, :, cut:width].rearrange("p t s -> p s t"),
                in1=disc_row[:, s0 + cut : s0 + width].unsqueeze(2).to_broadcast([P, width - cut, 4]),
                op=ALU.mult,
            )
            nc.vector.tensor_tensor(
                out=staged["y", u][:, 0:cut, :].rearrange("p (a i) t -> p a t i", i=4),
                in0=z[u][:, :, 0:cut].rearrange("p t (a i) -> p a t i", i=4),
                in1=disc_bank[:, s0 : s0 + cut].rearrange("p (a i) -> p a i", i=4).unsqueeze(2).to_broadcast([P, cut // 4, 4, 4]),
                op=ALU.mult,
            )

        def quantize_y(u):
            g, s0, width = units[u]
            if u != 6:
                y_words[u] = rotating("y_words", 4, [P, 384 if u == 5 else width], U32)
            words = y_words[5][:, 256:384] if u == 6 else y_words[u][:, 0:width]
            quantize(words, y_plane[:, g, s0 : s0 + width], staged["y", u][:].rearrange("p s t -> p (s t)"))

        def store_words(u):
            g, s0, width = units[u]
            width = y_words[u].shape[1]
            nc.sync.dma_start(
                out=out_1[g].rearrange("p s t -> p (s t)").bitcast(I32)[:, s0 : s0 + width], in_=y_words[u][:].bitcast(I32)
            )

        def store_scales(g0, g1, queues):
            for q in range(4):
                queues[q % len(queues)].dma_start(
                    out=out_2[g0:g1, q:16:4, :].rearrange("g r s -> r g s").bitcast(I32),
                    in_=y_plane[q:P:32, g0:g1, :].bitcast(I32),
                )

        turn_vectors()
        permute_w_plane()
        permute_w(0, 1)
        stage1(0, 0)
        group_n(0, 1)
        permute_w(1, 3)
        quantize_n(0, 0)
        group_n(0, 2)
        permute_w(3, 4)
        group_n(0, 3)
        hedge_columns()
        stage1(0, 1)
        group_v(0, 0)
        quantize_n(0, 1)
        quantize_v(0, 0)
        stage1(0, 2)
        stage1(0, 3)
        group_v(0, 1)
        group_n(1, 0)
        quantize_v(0, 1)
        for k in range(TG):
            stage1(1, k)

        scalar_quarters = {}

        def unit(u):
            for t in range(4):
                stage2(u, t)
                if (u, t) == (0, 0):
                    turn_discount()
                if (u, t) == (0, 2):
                    spread_discount()
                if t == 0 and 0 < u < 5:
                    turn_and_store(u - 1)
                for g, k, quarter in scalar_quarters.get((u, t), []):
                    group_n_quarter(g, k, quarter)

        group_n(1, 1)
        group_n_pair(1, 1)
        unit(0)
        quantize_n(1, 0)
        quantize_n(1, 1)
        group_v(1, 0)
        group_v(1, 1)
        quantize_v(1, 0)
        quantize_v(1, 1)
        group_y(0)
        group_n_pair(2, 0)
        group_n_pair(2, 1)
        quantize_n(2, 0)
        quantize_n(2, 1)
        quantize_y(0)
        unit(1)
        unit(2)
        group_y(1)
        group_y(2)
        quantize_y(1)
        quantize_y(2)
        unit(3)
        store_words(0)
        group_y(3)
        unit(4)
        store_words(1)
        store_words(2)
        group_y(4)
        quantize_y(3)
        quantize_y(4)
        stage2(5, 0)
        turn(4, 0, 3)
        discount_tile(4, 0)
        turn(4, 3, 4)
        discount_tile(4, 1)
        store_rows(4, 0, 2, nc.sync)
        discount_tile(4, 2)
        stage2(5, 1)
        discount_tile(4, 3)
        store_rows(4, 2, 4, nc.sync)
        store_words(3)
        stage2(5, 2)
        stage2(5, 3)
        store_words(4)
        group_y(5)
        stage2(6, 0)
        stage2(6, 1)
        stage2(6, 2)
        stage2(6, 3)
        turn(5, 0, 2)
        turn(6, 0, 1)
        group_y(6)
        quantize_y(5)
        quantize_y(6)
        discount_tile(5, 0)
        store_rows(5, 0, 1, nc.sync)
        discount_tile(5, 1)
        store_rows(5, 1, 2, nc.sync)
        discount_tile(6, 0)
        store_words(5)
        store_rows(6, 0, 1, nc.scalar)
        store_scales(0, 3, [nc.sync, nc.scalar])
